import numpy as np
import ml_dtypes


def mxq(x, axis, fmt="e4m3"):
    dtype, down = {"e4m3": (ml_dtypes.float8_e4m3fn, 7), "e5m2": (ml_dtypes.float8_e5m2, 14)}[fmt]
    v = np.moveaxis(np.asarray(x, np.float32).astype(ml_dtypes.bfloat16).astype(np.float64), axis, -1)
    blocks = v.reshape(v.shape[:-1] + (-1, 32))
    amax = np.abs(blocks).max(-1, keepdims=True)
    byte = np.maximum(np.where(amax > 0, np.frexp(amax)[1] - 1 + 127, 0) - down, 1)
    scale = np.exp2(byte - 127.0)
    codes = (blocks / scale).astype(np.float32).astype(dtype).astype(np.float64)
    return np.moveaxis((codes * scale).reshape(v.shape), -1, axis)


WIDE = False


def mx_kscale(k):
    if not WIDE:
        return np.ones(k)
    levels = np.array([10, -10, 5, -5, 0])
    if k % 512:
        return np.exp2(np.random.permutation(np.resize(levels, k // 32))).repeat(32)
    a = np.empty((k // 512, 16))
    for p in range(k // 512):
        a[p, :8] = np.random.permutation(np.resize(levels, 8))
        for g in range(8):
            far = levels[np.abs(levels - a[p, g]) >= 10]
            a[p, g + 8] = far[np.random.randint(len(far))]
    return np.exp2(a.ravel()).repeat(32)


def f64(x):
    return np.asarray(x).astype(np.float64)


def striped(idx):
    return np.tile(np.asarray(idx).reshape(-1, 16).T, (8, 1)).astype(np.uint16)


def unstriped(offs):
    return offs[:16].T.reshape(-1).astype(np.int64)


def sigmoid(v):
    return 1.0 / (1.0 + np.exp(-v))


D, T, I, Q, U, M = 512, 2048, 512, 128, 1024, 2048


def setup_inputs():
    n = np.random.standard_normal
    idx = np.random.permutation(T)[:I]
    idx2 = np.random.permutation(U)[:I]
    idx3 = np.random.permutation(M)[:I]
    fd = mx_kscale(D)
    return {
        "query": (n((D, Q)) * 0.9 / np.sqrt(D) * fd[:, None]).astype(np.float32),
        "keys": (n((D, T)) / fd[:, None]).astype(np.float32),
        "notes": (n((D, U)) / fd[:, None]).astype(np.float32),
        "old": (np.random.uniform(0.0, 2.0, (Q, M))).astype(np.float32),
        "fade": (np.random.uniform(0.3, 0.9, (Q, 1))).astype(np.float32),
        "offs": striped(idx),
        "offs2": striped(idx2),
        "offs3": striped(idx3),
    }


def reference(query, keys, notes, old, fade, offs, offs2, offs3):
    idx = unstriped(offs)
    idx2 = unstriped(offs2)
    idx3 = unstriped(offs3)
    zk = np.maximum(f64(keys)[:, idx], f64(notes)[:, idx2])
    queryq = mxq(f64(query), 0, "e4m3")
    zkq = mxq(zk, 0, "e4m3")
    s = queryq.T @ zkq
    w = sigmoid(s)
    ws = w * 2.0
    wf = np.zeros((Q, M))
    wf[:, idx3] = ws
    y = f64(old) * f64(fade) + wf
    return y

@@ -1,0 +1,126 @@
+from contextlib import ExitStack
+
+import concourse.mybir as mybir
+
+D, T, I, Q, U, M = 512, 2048, 512, 128, 1024, 2048
+FLOPS = 2 * D * Q * I
+
+F32 = mybir.dt.float32
+BF16 = mybir.dt.bfloat16
+U32 = mybir.dt.uint32
+U16 = mybir.dt.uint16
+U8 = mybir.dt.uint8
+FP8X4 = mybir.dt.float8_e4m3fn_x4
+ALU = mybir.AluOpType
+ACT = mybir.ActivationFunctionType
+
+P = 128
+PACK = 4
+LIST_ROWS = 16
+CHUNK = 128
+CHUNKS = I // CHUNK
+OUT_COLS = 512
+
+
+def tile_attend_keylarger_counts_lean_kernel(tc, query, keys, notes, old, fade, offs, offs2, offs3, out):
+    nc = tc.nc
+    with ExitStack() as ctx:
+        sb = ctx.enter_context(tc.tile_pool(name="sb", bufs=1))
+        psum = ctx.enter_context(tc.psum_pool(name="psum", bufs=1))
+
+        key_planes = keys.rearrange("(p j) t -> j p t", j=PACK)
+        note_planes = notes.rearrange("(p j) u -> j p u", j=PACK)
+        key_sb = [sb.tile([P, T], F32, name=f"key_sb{j}") for j in range(PACK)]
+        note_sb = [sb.tile([P, U], F32, name=f"note_sb{j}") for j in range(PACK)]
+        key_list = sb.tile([P, I // LIST_ROWS], U16, name="key_list")
+        note_list = sb.tile([P, I // LIST_ROWS], U16, name="note_list")
+        place_list = sb.tile([P, I // LIST_ROWS], U16, name="place_list")
+        query_sb = sb.tile([P, PACK, Q], F32, name="query_sb")
+        old_sb = sb.tile([P, M], F32, name="old_sb")
+        fade_sb = sb.tile([P, 1], F32, name="fade_sb")
+
+        nc.sync.dma_start(note_sb[0][:], note_planes[0])
+        nc.sync.dma_start(note_list[:], offs2)
+        nc.sync.dma_start(key_list[:], offs)
+        nc.sync.dma_start(key_sb[0][:], key_planes[0])
+        nc.sync.dma_start(query_sb[:], query.rearrange("(p j) q -> p j q", j=PACK))
+        for j in range(1, PACK):
+            nc.sync.dma_start(note_sb[j][:], note_planes[j])
+            nc.sync.dma_start(key_sb[j][:], key_planes[j])
+        nc.sync.dma_start(place_list[:], offs3)
+        nc.sync.dma_start(fade_sb[:], fade)
+        nc.sync.dma_start(old_sb[:], old)
+
+        placed = sb.tile([P, M], F32, name="placed")
+        nc.vector.memset(placed[:], 0.0)
+        ones = sb.tile([P, CHUNK], F32, name="ones")
+        nc.vector.memset(ones[:], 1.0)
+
+        larger = [sb.tile([P, CHUNK, PACK], BF16, name=f"larger{c}", align_bytes=64) for c in range(CHUNKS)]
+        picked_keys = [sb.tile([P, I], F32, name=f"picked_keys{j}") for j in range(PACK - 1)]
+        picked_notes = [sb.tile([P, I], F32, name=f"picked_notes{j}") for j in range(PACK)]
+        last_keys = [sb.tile([P, CHUNK], F32, name=f"last_keys{c}") for c in range(CHUNKS)]
+
+        def slots(c):
+            return slice(c * CHUNK, (c + 1) * CHUNK)
+
+        def entries(c):
+            return slice(c * CHUNK // LIST_ROWS, (c + 1) * CHUNK // LIST_ROWS)
+
+        query_bf = sb.tile([P, Q, PACK], BF16, name="query_bf", align_bytes=64)
+        query_codes = sb.tile([P, Q], U32, name="query_codes", align_bytes=64)
+        query_scales = sb.tile([P, Q], U8, name="query_scales", align_bytes=64)
+
+        for j in range(PACK - 1):
+            nc.vector.tensor_copy(picked_notes[j][:], note_sb[j][:].indirect(note_list[:]))
+            nc.scalar.activation(picked_keys[j][:], key_sb[j][:].indirect(key_list[:]), ACT.Copy)
+            for c in range(CHUNKS):
+                nc.vector.tensor_tensor(larger[c][:, :, j], picked_keys[j][:, slots(c)], picked_notes[j][:, slots(c)], ALU.max)
+            if j == 0:
+                nc.vector.tensor_copy(query_bf[:], query_sb[:].rearrange("p j q -> p q j"))
+                nc.vector.quantize_mx(
+                    out=query_codes[:].bitcast(FP8X4), scales=query_scales[:], in_=query_bf[:].rearrange("p q j -> p (q j)")
+                )
+
+        last = PACK - 1
+        nc.scalar.activation(picked_notes[last][:], note_sb[last][:].indirect(note_list[:]), ACT.Copy)
+        for c in range(CHUNKS):
+            nc.scalar.activation(last_keys[c][:], key_sb[last][:].indirect(key_list[:, entries(c)]), ACT.Copy)
+
+        codes = [sb.tile([P, CHUNK], U32, name=f"codes{c}", align_bytes=64) for c in range(CHUNKS)]
+        scales = [sb.tile([P, CHUNK], U8, name=f"scales{c}", align_bytes=64) for c in range(CHUNKS)]
+        scores = [psum.tile([P, CHUNK], F32, name=f"scores{c}") for c in range(CHUNKS)]
+        half_tanh = [sb.tile([P, CHUNK], F32, name=f"half_tanh{c}") for c in range(CHUNKS)]
+
+        def finish_keys(c):
+            nc.vector.tensor_tensor(larger[c][:, :, last], last_keys[c][:], picked_notes[last][:, slots(c)], ALU.max)
+
+        def score(c):
+            nc.vector.quantize_mx(
+                out=codes[c][:].bitcast(FP8X4), scales=scales[c][:], in_=larger[c][:].rearrange("p i j -> p (i j)")
+            )
+            nc.tensor.matmul_mx(
+                out=scores[c][:],
+                lhsT=query_codes[:].bitcast(FP8X4),
+                lhsT_scale=query_scales[:],
+                rhs=codes[c][:].bitcast(FP8X4),
+                rhs_scale=scales[c][:],
+                start=True,
+                stop=True,
+            )
+            nc.scalar.activation(half_tanh[c][:], scores[c][:], ACT.Tanh, scale=0.5)
+
+        finish_keys(0)
+        for c in range(1, CHUNKS):
+            finish_keys(c)
+            score(c - 1)
+        score(CHUNKS - 1)
+
+        for c in range(CHUNKS):
+            nc.vector.tensor_tensor(placed[:].indirect(place_list[:, entries(c)]), half_tanh[c][:], ones[:], ALU.add)
+
+        for b in range(M // OUT_COLS):
+            cols = slice(b * OUT_COLS, (b + 1) * OUT_COLS)
+            result = sb.tile([P, OUT_COLS], F32, name=f"result{b}")
+            nc.vector.scalar_tensor_tensor(result[:], old_sb[:, cols], fade_sb[:], placed[:, cols], ALU.mult, ALU.add)
+            nc.sync.dma_start(out[:, cols], result[:])

@@ -19,7 +19,8 @@ PACK = 4
 LIST_ROWS = 16
 CHUNK = 128
 CHUNKS = I // CHUNK
-OUT_COLS = 512
+HALF = I // 2
+OUT_WIDTHS = (256, 512, 512, 512, 256)
 
 
 def tile_attend_keylarger_counts_lean_kernel(tc, query, keys, notes, old, fade, offs, offs2, offs3, out):
@@ -44,22 +45,24 @@ def tile_attend_keylarger_counts_lean_kernel(tc, query, keys, notes, old, fade, 
         nc.sync.dma_start(key_list[:], offs)
         nc.sync.dma_start(key_sb[0][:], key_planes[0])
         nc.sync.dma_start(query_sb[:], query.rearrange("(p j) q -> p j q", j=PACK))
-        for j in range(1, PACK):
-            nc.sync.dma_start(note_sb[j][:], note_planes[j])
-            nc.sync.dma_start(key_sb[j][:], key_planes[j])
+        nc.sync.dma_start(note_sb[1][:], note_planes[1])
+        nc.sync.dma_start(note_sb[2][:], note_planes[2])
+        nc.sync.dma_start(key_sb[1][:], key_planes[1])
+        nc.sync.dma_start(key_sb[2][:], key_planes[2])
+        nc.sync.dma_start(note_sb[3][:], note_planes[3])
+        nc.sync.dma_start(key_sb[3][:], key_planes[3])
         nc.sync.dma_start(place_list[:], offs3)
         nc.sync.dma_start(fade_sb[:], fade)
         nc.sync.dma_start(old_sb[:], old)
 
         placed = sb.tile([P, M], F32, name="placed")
         nc.vector.memset(placed[:], 0.0)
-        ones = sb.tile([P, CHUNK], F32, name="ones")
+        ones = sb.tile([P, HALF], F32, name="ones")
         nc.vector.memset(ones[:], 1.0)
 
         larger = [sb.tile([P, CHUNK, PACK], BF16, name=f"larger{c}", align_bytes=64) for c in range(CHUNKS)]
-        picked_keys = [sb.tile([P, I], F32, name=f"picked_keys{j}") for j in range(PACK - 1)]
+        picked_keys = [[sb.tile([P, CHUNK], F32, name=f"picked_keys{j}_{c}") for c in range(CHUNKS)] for j in range(PACK)]
         picked_notes = [sb.tile([P, I], F32, name=f"picked_notes{j}") for j in range(PACK)]
-        last_keys = [sb.tile([P, CHUNK], F32, name=f"last_keys{c}") for c in range(CHUNKS)]
 
         def slots(c):
             return slice(c * CHUNK, (c + 1) * CHUNK)
@@ -71,29 +74,31 @@ def tile_attend_keylarger_counts_lean_kernel(tc, query, keys, notes, old, fade, 
         query_codes = sb.tile([P, Q], U32, name="query_codes", align_bytes=64)
         query_scales = sb.tile([P, Q], U8, name="query_scales", align_bytes=64)
 
-        for j in range(PACK - 1):
-            nc.vector.tensor_copy(picked_notes[j][:], note_sb[j][:].indirect(note_list[:]))
-            nc.scalar.activation(picked_keys[j][:], key_sb[j][:].indirect(key_list[:]), ACT.Copy)
+        def pick(j):
+            nc.scalar.activation(picked_notes[j][:], note_sb[j][:].indirect(note_list[:]), ACT.Copy)
+            nc.vector.tensor_copy(picked_keys[j][0][:], key_sb[j][:].indirect(key_list[:, entries(0)]))
+            for c in range(1, CHUNKS):
+                nc.scalar.activation(picked_keys[j][c][:], key_sb[j][:].indirect(key_list[:, entries(c)]), ACT.Copy)
+
+        def take_larger(j, c):
+            nc.vector.tensor_tensor(larger[c][:, :, j], picked_keys[j][c][:], picked_notes[j][:, slots(c)], ALU.max)
+
+        last = PACK - 1
+        for j in range(last):
+            pick(j)
             for c in range(CHUNKS):
-                nc.vector.tensor_tensor(larger[c][:, :, j], picked_keys[j][:, slots(c)], picked_notes[j][:, slots(c)], ALU.max)
+                take_larger(j, c)
             if j == 0:
                 nc.vector.tensor_copy(query_bf[:], query_sb[:].rearrange("p j q -> p q j"))
                 nc.vector.quantize_mx(
                     out=query_codes[:].bitcast(FP8X4), scales=query_scales[:], in_=query_bf[:].rearrange("p q j -> p (q j)")
                 )
-
-        last = PACK - 1
-        nc.scalar.activation(picked_notes[last][:], note_sb[last][:].indirect(note_list[:]), ACT.Copy)
-        for c in range(CHUNKS):
-            nc.scalar.activation(last_keys[c][:], key_sb[last][:].indirect(key_list[:, entries(c)]), ACT.Copy)
+        pick(last)
 
         codes = [sb.tile([P, CHUNK], U32, name=f"codes{c}", align_bytes=64) for c in range(CHUNKS)]
         scales = [sb.tile([P, CHUNK], U8, name=f"scales{c}", align_bytes=64) for c in range(CHUNKS)]
         scores = [psum.tile([P, CHUNK], F32, name=f"scores{c}") for c in range(CHUNKS)]
-        half_tanh = [sb.tile([P, CHUNK], F32, name=f"half_tanh{c}") for c in range(CHUNKS)]
-
-        def finish_keys(c):
-            nc.vector.tensor_tensor(larger[c][:, :, last], last_keys[c][:], picked_notes[last][:, slots(c)], ALU.max)
+        half_tanh = sb.tile([P, I], F32, name="half_tanh")
 
         def score(c):
             nc.vector.quantize_mx(
@@ -108,19 +113,24 @@ def tile_attend_keylarger_counts_lean_kernel(tc, query, keys, notes, old, fade, 
                 start=True,
                 stop=True,
             )
-            nc.scalar.activation(half_tanh[c][:], scores[c][:], ACT.Tanh, scale=0.5)
+            nc.scalar.activation(half_tanh[:, slots(c)], scores[c][:], ACT.Tanh, scale=0.5)
 
-        finish_keys(0)
-        for c in range(1, CHUNKS):
-            finish_keys(c)
-            score(c - 1)
-        score(CHUNKS - 1)
+        for pair in range(0, CHUNKS, 2):
+            take_larger(last, pair)
+            take_larger(last, pair + 1)
+            score(pair)
+            score(pair + 1)
 
-        for c in range(CHUNKS):
-            nc.vector.tensor_tensor(placed[:].indirect(place_list[:, entries(c)]), half_tanh[c][:], ones[:], ALU.add)
+        for h in range(I // HALF):
+            half_entries = slice(h * HALF // LIST_ROWS, (h + 1) * HALF // LIST_ROWS)
+            nc.vector.tensor_tensor(
+                placed[:].indirect(place_list[:, half_entries]), half_tanh[:, h * HALF : (h + 1) * HALF], ones[:], ALU.add
+            )
 
-        for b in range(M // OUT_COLS):
-            cols = slice(b * OUT_COLS, (b + 1) * OUT_COLS)
-            result = sb.tile([P, OUT_COLS], F32, name=f"result{b}")
+        first = 0
+        for b, width in enumerate(OUT_WIDTHS):
+            cols = slice(first, first + width)
+            first = first + width
+            result = sb.tile([P, width], F32, name=f"result{b}")
             nc.vector.scalar_tensor_tensor(result[:], old_sb[:, cols], fade_sb[:], placed[:, cols], ALU.mult, ALU.add)
             nc.sync.dma_start(out[:, cols], result[:])

@@ -19,7 +19,6 @@ PACK = 4
 LIST_ROWS = 16
 CHUNK = 128
 CHUNKS = I // CHUNK
-HALF = I // 2
 OUT_WIDTHS = (256, 512, 512, 512, 256)
 
 
@@ -36,7 +35,7 @@ def tile_attend_keylarger_counts_lean_kernel(tc, query, keys, notes, old, fade, 
         key_list = sb.tile([P, I // LIST_ROWS], U16, name="key_list")
         note_list = sb.tile([P, I // LIST_ROWS], U16, name="note_list")
         place_list = sb.tile([P, I // LIST_ROWS], U16, name="place_list")
-        query_sb = sb.tile([P, PACK, Q], F32, name="query_sb")
+        query_sb = sb.tile([P, PACK, Q], F32, name="query_sb", tag="query_then_keys")
         old_sb = sb.tile([P, M], F32, name="old_sb")
         fade_sb = sb.tile([P, 1], F32, name="fade_sb")
 
@@ -44,24 +43,24 @@ def tile_attend_keylarger_counts_lean_kernel(tc, query, keys, notes, old, fade, 
         nc.sync.dma_start(note_list[:], offs2)
         nc.sync.dma_start(key_list[:], offs)
         nc.sync.dma_start(key_sb[0][:], key_planes[0])
-        nc.sync.dma_start(query_sb[:], query.rearrange("(p j) q -> p j q", j=PACK))
         nc.sync.dma_start(note_sb[1][:], note_planes[1])
         nc.sync.dma_start(note_sb[2][:], note_planes[2])
         nc.sync.dma_start(key_sb[1][:], key_planes[1])
         nc.sync.dma_start(key_sb[2][:], key_planes[2])
         nc.sync.dma_start(note_sb[3][:], note_planes[3])
         nc.sync.dma_start(key_sb[3][:], key_planes[3])
+        nc.sync.dma_start(query_sb[:], query.rearrange("(p j) q -> p j q", j=PACK))
         nc.sync.dma_start(place_list[:], offs3)
         nc.sync.dma_start(fade_sb[:], fade)
         nc.sync.dma_start(old_sb[:], old)
 
         placed = sb.tile([P, M], F32, name="placed")
         nc.vector.memset(placed[:], 0.0)
-        ones = sb.tile([P, HALF], F32, name="ones")
+        ones = sb.tile([P, I // 2], F32, name="ones")
         nc.vector.memset(ones[:], 1.0)
 
         larger = [sb.tile([P, CHUNK, PACK], BF16, name=f"larger{c}", align_bytes=64) for c in range(CHUNKS)]
-        picked_keys = [[sb.tile([P, CHUNK], F32, name=f"picked_keys{j}_{c}") for c in range(CHUNKS)] for j in range(PACK)]
+        picked_keys = [[sb.tile([P, CHUNK], F32, name=f"picked_keys{j}_{c}") for c in range(CHUNKS)] for j in range(PACK - 1)]
         picked_notes = [sb.tile([P, I], F32, name=f"picked_notes{j}") for j in range(PACK)]
 
         def slots(c):
@@ -74,10 +73,15 @@ def tile_attend_keylarger_counts_lean_kernel(tc, query, keys, notes, old, fade, 
         query_codes = sb.tile([P, Q], U32, name="query_codes", align_bytes=64)
         query_scales = sb.tile([P, Q], U8, name="query_scales", align_bytes=64)
 
-        def pick(j):
+        def pick_notes(j):
             nc.scalar.activation(picked_notes[j][:], note_sb[j][:].indirect(note_list[:]), ACT.Copy)
-            nc.vector.tensor_copy(picked_keys[j][0][:], key_sb[j][:].indirect(key_list[:, entries(0)]))
-            for c in range(1, CHUNKS):
+
+        def pick_keys_on_vector(j):
+            for c in range(CHUNKS // 2):
+                nc.vector.tensor_copy(picked_keys[j][c][:], key_sb[j][:].indirect(key_list[:, entries(c)]))
+
+        def pick_keys_on_scalar(j):
+            for c in range(CHUNKS // 2, CHUNKS):
                 nc.scalar.activation(picked_keys[j][c][:], key_sb[j][:].indirect(key_list[:, entries(c)]), ACT.Copy)
 
         def take_larger(j, c):
@@ -85,15 +89,22 @@ def tile_attend_keylarger_counts_lean_kernel(tc, query, keys, notes, old, fade, 
 
         last = PACK - 1
         for j in range(last):
-            pick(j)
+            pick_notes(j)
+            pick_keys_on_vector(j)
+            pick_keys_on_scalar(j)
             for c in range(CHUNKS):
                 take_larger(j, c)
-            if j == 0:
-                nc.vector.tensor_copy(query_bf[:], query_sb[:].rearrange("p j q -> p q j"))
-                nc.vector.quantize_mx(
-                    out=query_codes[:].bitcast(FP8X4), scales=query_scales[:], in_=query_bf[:].rearrange("p q j -> p (q j)")
-                )
-        pick(last)
+        pick_notes(last)
+        picked_keys.append([sb.tile([P, CHUNK], F32, name=f"picked_keys{last}_{c}") for c in range(CHUNKS // 2)])
+        pick_keys_on_vector(last)
+        nc.scalar.copy(query_bf[:], query_sb[:].rearrange("p j q -> p q j"))
+        nc.vector.quantize_mx(
+            out=query_codes[:].bitcast(FP8X4), scales=query_scales[:], in_=query_bf[:].rearrange("p q j -> p (q j)")
+        )
+
+        late_keys = sb.tile([P, I // 2], F32, name="late_keys", tag="query_then_keys")
+        picked_keys[last].extend([late_keys[:, slots(c)] for c in range(CHUNKS // 2)])
+        pick_keys_on_scalar(last)
 
         codes = [sb.tile([P, CHUNK], U32, name=f"codes{c}", align_bytes=64) for c in range(CHUNKS)]
         scales = [sb.tile([P, CHUNK], U8, name=f"scales{c}", align_bytes=64) for c in range(CHUNKS)]
@@ -121,10 +132,12 @@ def tile_attend_keylarger_counts_lean_kernel(tc, query, keys, notes, old, fade, 
             score(pair)
             score(pair + 1)
 
-        for h in range(I // HALF):
-            half_entries = slice(h * HALF // LIST_ROWS, (h + 1) * HALF // LIST_ROWS)
+        for lo, hi in ((0, I // 2), (I // 2, I)):
             nc.vector.tensor_tensor(
-                placed[:].indirect(place_list[:, half_entries]), half_tanh[:, h * HALF : (h + 1) * HALF], ones[:], ALU.add
+                placed[:].indirect(place_list[:, lo // LIST_ROWS : hi // LIST_ROWS]),
+                half_tanh[:, lo:hi],
+                ones[:, : hi - lo],
+                ALU.add,
             )
 
         first = 0

from contextlib import ExitStack

import concourse.mybir as mybir

D, T, I, Q, U, M = 512, 2048, 512, 128, 1024, 2048
FLOPS = 2 * D * Q * I

F32 = mybir.dt.float32
BF16 = mybir.dt.bfloat16
U32 = mybir.dt.uint32
U16 = mybir.dt.uint16
U8 = mybir.dt.uint8
FP8X4 = mybir.dt.float8_e4m3fn_x4
ALU = mybir.AluOpType
ACT = mybir.ActivationFunctionType

P = 128
PACK = 4
LIST_ROWS = 16
CHUNK = 128
CHUNKS = I // CHUNK
OUT_WIDTHS = (256, 512, 512, 512, 256)


def tile_attend_keylarger_counts_lean_kernel(tc, query, keys, notes, old, fade, offs, offs2, offs3, out):
    nc = tc.nc
    with ExitStack() as ctx:
        sb = ctx.enter_context(tc.tile_pool(name="sb", bufs=1))
        psum = ctx.enter_context(tc.psum_pool(name="psum", bufs=1))

        key_planes = keys.rearrange("(p j) t -> j p t", j=PACK)
        note_planes = notes.rearrange("(p j) u -> j p u", j=PACK)
        key_sb = [sb.tile([P, T], F32, name=f"key_sb{j}") for j in range(PACK)]
        note_sb = [sb.tile([P, U], F32, name=f"note_sb{j}") for j in range(PACK)]
        key_list = sb.tile([P, I // LIST_ROWS], U16, name="key_list")
        note_list = sb.tile([P, I // LIST_ROWS], U16, name="note_list")
        place_list = sb.tile([P, I // LIST_ROWS], U16, name="place_list")
        query_sb = sb.tile([P, PACK, Q], F32, name="query_sb", tag="query_then_keys")
        old_sb = sb.tile([P, M], F32, name="old_sb")
        fade_sb = sb.tile([P, 1], F32, name="fade_sb")

        nc.sync.dma_start(note_sb[0][:], note_planes[0])
        nc.sync.dma_start(note_list[:], offs2)
        nc.sync.dma_start(key_list[:], offs)
        nc.sync.dma_start(key_sb[0][:], key_planes[0])
        nc.sync.dma_start(note_sb[1][:], note_planes[1])
        nc.sync.dma_start(note_sb[2][:], note_planes[2])
        nc.sync.dma_start(key_sb[1][:], key_planes[1])
        nc.sync.dma_start(key_sb[2][:], key_planes[2])
        nc.sync.dma_start(note_sb[3][:], note_planes[3])
        nc.sync.dma_start(key_sb[3][:], key_planes[3])
        nc.sync.dma_start(query_sb[:], query.rearrange("(p j) q -> p j q", j=PACK))
        nc.sync.dma_start(place_list[:], offs3)
        nc.sync.dma_start(fade_sb[:], fade)
        nc.sync.dma_start(old_sb[:], old)

        placed = sb.tile([P, M], F32, name="placed")
        nc.vector.memset(placed[:], 0.0)
        ones = sb.tile([P, I // 2], F32, name="ones")
        nc.vector.memset(ones[:], 1.0)

        larger = [sb.tile([P, CHUNK, PACK], BF16, name=f"larger{c}", align_bytes=64) for c in range(CHUNKS)]
        picked_keys = [[sb.tile([P, CHUNK], F32, name=f"picked_keys{j}_{c}") for c in range(CHUNKS)] for j in range(PACK - 1)]
        picked_notes = [sb.tile([P, I], F32, name=f"picked_notes{j}") for j in range(PACK)]

        def slots(c):
            return slice(c * CHUNK, (c + 1) * CHUNK)

        def entries(c):
            return slice(c * CHUNK // LIST_ROWS, (c + 1) * CHUNK // LIST_ROWS)

        query_bf = sb.tile([P, Q, PACK], BF16, name="query_bf", align_bytes=64)
        query_codes = sb.tile([P, Q], U32, name="query_codes", align_bytes=64)
        query_scales = sb.tile([P, Q], U8, name="query_scales", align_bytes=64)

        def pick_notes(j):
            nc.scalar.activation(picked_notes[j][:], note_sb[j][:].indirect(note_list[:]), ACT.Copy)

        def pick_keys_on_vector(j):
            for c in range(CHUNKS // 2):
                nc.vector.tensor_copy(picked_keys[j][c][:], key_sb[j][:].indirect(key_list[:, entries(c)]))

        def pick_keys_on_scalar(j):
            for c in range(CHUNKS // 2, CHUNKS):
                nc.scalar.activation(picked_keys[j][c][:], key_sb[j][:].indirect(key_list[:, entries(c)]), ACT.Copy)

        def take_larger(j, c):
            nc.vector.tensor_tensor(larger[c][:, :, j], picked_keys[j][c][:], picked_notes[j][:, slots(c)], ALU.max)

        last = PACK - 1
        for j in range(last):
            pick_notes(j)
            pick_keys_on_vector(j)
            pick_keys_on_scalar(j)
            for c in range(CHUNKS):
                take_larger(j, c)
        pick_notes(last)
        picked_keys.append([sb.tile([P, CHUNK], F32, name=f"picked_keys{last}_{c}") for c in range(CHUNKS // 2)])
        pick_keys_on_vector(last)
        nc.scalar.copy(query_bf[:], query_sb[:].rearrange("p j q -> p q j"))
        nc.vector.quantize_mx(
            out=query_codes[:].bitcast(FP8X4), scales=query_scales[:], in_=query_bf[:].rearrange("p q j -> p (q j)")
        )

        late_keys = sb.tile([P, I // 2], F32, name="late_keys", tag="query_then_keys")
        picked_keys[last].extend([late_keys[:, slots(c)] for c in range(CHUNKS // 2)])
        pick_keys_on_scalar(last)

        codes = [sb.tile([P, CHUNK], U32, name=f"codes{c}", align_bytes=64) for c in range(CHUNKS)]
        scales = [sb.tile([P, CHUNK], U8, name=f"scales{c}", align_bytes=64) for c in range(CHUNKS)]
        scores = [psum.tile([P, CHUNK], F32, name=f"scores{c}") for c in range(CHUNKS)]
        half_tanh = sb.tile([P, I], F32, name="half_tanh")

        def score(c):
            nc.vector.quantize_mx(
                out=codes[c][:].bitcast(FP8X4), scales=scales[c][:], in_=larger[c][:].rearrange("p i j -> p (i j)")
            )
            nc.tensor.matmul_mx(
                out=scores[c][:],
                lhsT=query_codes[:].bitcast(FP8X4),
                lhsT_scale=query_scales[:],
                rhs=codes[c][:].bitcast(FP8X4),
                rhs_scale=scales[c][:],
                start=True,
                stop=True,
            )
            nc.scalar.activation(half_tanh[:, slots(c)], scores[c][:], ACT.Tanh, scale=0.5)

        for pair in range(0, CHUNKS, 2):
            take_larger(last, pair)
            take_larger(last, pair + 1)
            score(pair)
            score(pair + 1)

        for lo, hi in ((0, I // 2), (I // 2, I)):
            nc.vector.tensor_tensor(
                placed[:].indirect(place_list[:, lo // LIST_ROWS : hi // LIST_ROWS]),
                half_tanh[:, lo:hi],
                ones[:, : hi - lo],
                ALU.add,
            )

        first = 0
        for b, width in enumerate(OUT_WIDTHS):
            cols = slice(first, first + width)
            first = first + width
            result = sb.tile([P, width], F32, name=f"result{b}")
            nc.vector.scalar_tensor_tensor(result[:], old_sb[:, cols], fade_sb[:], placed[:, cols], ALU.mult, ALU.add)
            nc.sync.dma_start(out[:, cols], result[:])
